import numpy as np
import ml_dtypes


def mxq(x, axis, fmt="e4m3"):
    dtype, down = {"e4m3": (ml_dtypes.float8_e4m3fn, 7), "e5m2": (ml_dtypes.float8_e5m2, 14)}[fmt]
    v = np.moveaxis(np.asarray(x, np.float32).astype(ml_dtypes.bfloat16).astype(np.float64), axis, -1)
    blocks = v.reshape(v.shape[:-1] + (-1, 32))
    amax = np.abs(blocks).max(-1, keepdims=True)
    byte = np.maximum(np.where(amax > 0, np.frexp(amax)[1] - 1 + 127, 0) - down, 1)
    scale = np.exp2(byte - 127.0)
    codes = (blocks / scale).astype(np.float32).astype(dtype).astype(np.float64)
    return np.moveaxis((codes * scale).reshape(v.shape), -1, axis)


WIDE = False


def mx_kscale(k):
    if not WIDE:
        return np.ones(k)
    levels = np.array([10, -10, 5, -5, 0])
    if k % 512:
        return np.exp2(np.random.permutation(np.resize(levels, k // 32))).repeat(32)
    a = np.empty((k // 512, 16))
    for p in range(k // 512):
        a[p, :8] = np.random.permutation(np.resize(levels, 8))
        for g in range(8):
            far = levels[np.abs(levels - a[p, g]) >= 10]
            a[p, g + 8] = far[np.random.randint(len(far))]
    return np.exp2(a.ravel()).repeat(32)


def f64(x):
    return np.asarray(x).astype(np.float64)


def striped(idx):
    return np.tile(idx.reshape(-1, 16).T, (8, 1)).astype(np.uint16)


def unstriped(offs):
    return offs[:16].T.reshape(-1).astype(np.int64)


def pack_weight(w):
    k, n = w.shape
    w = f64(np.asarray(w, np.float32).astype(ml_dtypes.bfloat16)).reshape(k // 32, 32, n)
    amax = np.abs(w).max(1)
    byte = np.clip(np.where(amax > 0, np.frexp(amax)[1] - 1 + 127 - 7, 1), 1, 254)
    scaled = (w * np.exp2(127.0 - byte)[:, None, :]).reshape(k, n).astype(np.float32)
    words = np.ascontiguousarray(scaled.reshape(k // 512, 128, 4, n).transpose(0, 1, 3, 2)).astype(ml_dtypes.float8_e4m3fn).view(np.uint8)
    return words, np.ascontiguousarray(byte.astype(np.uint8).reshape(k // 512, 16, n))


def unpack_weight(words, scales):
    g, p, n, _ = words.shape
    vals = np.ascontiguousarray(words).view(ml_dtypes.float8_e4m3fn).astype(np.float64) * np.repeat(np.exp2(scales.astype(np.float64) - 127.0), 8, axis=1)[..., None]
    return vals.transpose(0, 1, 3, 2).reshape(g * 512, n)


K, T, E, C, N = 512, 1024, 8, 128, 256


def by_expert(wq, xq):
    return np.concatenate([wq[e].T @ xq[:, e * C:(e + 1) * C] for e in range(E)], axis=1)


def setup_inputs():
    n = np.random.standard_normal
    s = mx_kscale(K)[:, None]
    packed = [pack_weight(m) for m in n((E, K, N)) / np.sqrt(K) / s[None]]
    return {
        "xT": (n((K, T)) * s).astype(np.float32),
        "w_words": np.stack([m[0] for m in packed]),
        "w_scales": np.stack([m[1] for m in packed]),
        "gate": np.tile(np.random.uniform(0.2, 1.0, E * C), (N, 1)).astype(np.float32),
        "offs": striped(np.random.permutation(T)[:E * C]),
    }


def reference(xT, w_words, w_scales, gate, offs):
    idx = unstriped(offs)
    xq = mxq(f64(xT)[:, idx], 0, "e4m3")
    w = np.stack([unpack_weight(w_words[e], w_scales[e]) for e in range(E)])
    y = by_expert(w, xq)
    out = np.zeros((N, T))
    out[:, idx] = f64(gate) * y
    return out

@@ -1,0 +1,105 @@
+from contextlib import ExitStack
+
+import concourse.mybir as mybir
+
+K, T, E, C, N = 512, 1024, 8, 128, 256
+FLOPS = 2 * K * N * E * C
+
+F32 = mybir.dt.float32
+BF16 = mybir.dt.bfloat16
+U32 = mybir.dt.uint32
+I32 = mybir.dt.int32
+U16 = mybir.dt.uint16
+U8 = mybir.dt.uint8
+FP8X4 = mybir.dt.float8_e4m3fn_x4
+MULT = mybir.AluOpType.mult
+
+P = 128
+PACK = 4
+PIECE = 512
+PIECES = E * C // PIECE
+EXPERTS = PIECE // C
+HALVES = N // P
+
+
+def tile_routed_moe_kernel(tc, xT, w_words, w_scales, gate, offs, out):
+    nc = tc.nc
+    with ExitStack() as ctx:
+        lists = ctx.enter_context(tc.tile_pool(name="lists", bufs=1))
+        held = ctx.enter_context(tc.tile_pool(name="held", bufs=1))
+        psum = ctx.enter_context(tc.psum_pool(name="psum", bufs=1))
+
+        offsets = lists.tile([P, E * C // 16], U16, name="offsets")
+        nc.sync.dma_start(offsets[:], offs)
+
+        x_rows = xT.rearrange("(g p t) n -> g p t n", p=P, t=PACK)
+        planes = []
+        for t in range(PACK):
+            plane = held.tile([P, T], F32, name="plane%d" % t)
+            nc.sync.dma_start(plane[:], x_rows[0, :, t, :])
+            planes.append(plane)
+
+        w_scale_sb = held.tile([P, E, N], U8, name="w_scale_sb", align_bytes=64)
+        nc.vector.memset(w_scale_sb[:].rearrange("p e n -> p (e n)").bitcast(I32), 0)
+        for q in range(4):
+            nc.sync.dma_start(
+                w_scale_sb[32 * q : 32 * q + 4, :, :].bitcast(I32),
+                w_scales[:, 0, 4 * q : 4 * q + 4, :].rearrange("e r n -> r e n").bitcast(I32),
+            )
+        w_code_sb = held.tile([P, E, N], U32, name="w_code_sb", align_bytes=64)
+        w_code_dram = w_words.rearrange("e a p n r -> p (e a) (n r)").bitcast(I32)
+        for i in range(PIECES):
+            es = slice(i * EXPERTS, (i + 1) * EXPERTS)
+            nc.sync.dma_start(w_code_sb[:, es, :].bitcast(I32), w_code_dram[:, es, :])
+
+        gates = []
+        for h in range(HALVES):
+            gate_sb = held.tile([P, E * C], F32, name="gate%d" % h)
+            nc.sync.dma_start(gate_sb[:], gate[h * P : (h + 1) * P, :])
+            gates.append(gate_sb)
+
+        windows = [held.tile([P, T], F32, name="window%d" % h) for h in range(HALVES)]
+
+        sums = {}
+        for i in range(PIECES):
+            cols = slice(i * PIECE // 16, (i + 1) * PIECE // 16)
+            picked = held.tile([P, PACK, PIECE], F32, name="picked%d" % i)
+            for t in range(PACK):
+                nc.vector.tensor_copy(picked[:, t, :], planes[t][:].indirect(offsets[:, cols]))
+            grouped = held.tile([P, PIECE, PACK], BF16, name="grouped%d" % i, align_bytes=64)
+            nc.scalar.copy(grouped[:], picked[:].rearrange("p t n -> p n t"))
+            x_code = held.tile([P, PIECE], U32, name="x_code%d" % i, align_bytes=64)
+            x_scale = held.tile([P, PIECE], U8, name="x_scale%d" % i, align_bytes=64)
+            nc.vector.quantize_mx(
+                out=x_code[:].bitcast(FP8X4),
+                scales=x_scale[:],
+                in_=grouped[:].rearrange("p n t -> p (n t)"),
+            )
+            for h in range(HALVES):
+                acc = psum.tile([P, PIECE], F32, name="acc%d_%d" % (i, h))
+                for j in range(EXPERTS):
+                    e = i * EXPERTS + j
+                    nc.tensor.matmul_mx(
+                        out=acc[:, j * C : (j + 1) * C],
+                        lhsT=w_code_sb[:, e, h * P : (h + 1) * P].bitcast(FP8X4),
+                        lhsT_scale=w_scale_sb[:, e, h * P : (h + 1) * P],
+                        rhs=x_code[:, j * C : (j + 1) * C].bitcast(FP8X4),
+                        rhs_scale=x_scale[:, j * C : (j + 1) * C],
+                        start=True,
+                        stop=True,
+                    )
+                y_sb = held.tile([P, PIECE], F32, name="y%d_%d" % (i, h))
+                nc.scalar.copy(y_sb[:], acc[:])
+                sums[(i, h)] = y_sb
+
+        for i in range(PIECES):
+            cols = slice(i * PIECE // 16, (i + 1) * PIECE // 16)
+            for h in range(HALVES):
+                nc.vector.tensor_tensor(
+                    windows[h][:].indirect(offsets[:, cols]),
+                    sums[(i, h)][:],
+                    gates[h][:, i * PIECE : (i + 1) * PIECE],
+                    MULT,
+                )
+        for h in range(HALVES):
+            nc.sync.dma_start(out[h * P : (h + 1) * P, :], windows[h][:])

@@ -13,13 +13,16 @@ U16 = mybir.dt.uint16
 U8 = mybir.dt.uint8
 FP8X4 = mybir.dt.float8_e4m3fn_x4
 MULT = mybir.AluOpType.mult
+COPY = mybir.ActivationFunctionType.Copy
 
 P = 128
 PACK = 4
-PIECE = 512
-PIECES = E * C // PIECE
-EXPERTS = PIECE // C
 HALVES = N // P
+
+SLICES = [(0, 256), (256, 256), (512, 256), (768, 256)]
+PIECES = [(0, 256), (256, 256), (512, 512)]
+ORDER = """c0 c1 c2 c3 g00 g10 g01 g11 g02 g12 g03 v0 g13 q0 m0 y00 y01 v1 q1 m1 y10 y11
+G20 G21 G22 G23 q2 m2 G30 G31 G32 G33 q3 m3 y20 y21 s00 s01 s10 s11 s20 o0 s21 o1"""
 
 
 def tile_routed_moe_kernel(tc, xT, w_words, w_scales, gate, offs, out):
@@ -41,65 +44,82 @@ def tile_routed_moe_kernel(tc, xT, w_words, w_scales, gate, offs, out):
 
         w_scale_sb = held.tile([P, E, N], U8, name="w_scale_sb", align_bytes=64)
         nc.vector.memset(w_scale_sb[:].rearrange("p e n -> p (e n)").bitcast(I32), 0)
-        for q in range(4):
-            nc.sync.dma_start(
-                w_scale_sb[32 * q : 32 * q + 4, :, :].bitcast(I32),
-                w_scales[:, 0, 4 * q : 4 * q + 4, :].rearrange("e r n -> r e n").bitcast(I32),
-            )
         w_code_sb = held.tile([P, E, N], U32, name="w_code_sb", align_bytes=64)
         w_code_dram = w_words.rearrange("e a p n r -> p (e a) (n r)").bitcast(I32)
-        for i in range(PIECES):
-            es = slice(i * EXPERTS, (i + 1) * EXPERTS)
-            nc.sync.dma_start(w_code_sb[:, es, :].bitcast(I32), w_code_dram[:, es, :])
-
+        gate_dram = gate.rearrange("(h p) j -> p h j", p=P)
         gates = []
-        for h in range(HALVES):
-            gate_sb = held.tile([P, E * C], F32, name="gate%d" % h)
-            nc.sync.dma_start(gate_sb[:], gate[h * P : (h + 1) * P, :])
+        for k, (s0, n) in enumerate(PIECES):
+            for q in range(4):
+                nc.sync.dma_start(
+                    w_scale_sb[32 * q : 32 * q + 4, s0 // C : (s0 + n) // C, :].bitcast(I32),
+                    w_scales[s0 // C : (s0 + n) // C, 0, 4 * q : 4 * q + 4, :].rearrange("e r n -> r e n").bitcast(I32),
+                )
+            nc.sync.dma_start(w_code_sb[:, s0 // C : (s0 + n) // C, :].bitcast(I32), w_code_dram[:, s0 // C : (s0 + n) // C, :])
+            gate_sb = held.tile([P, HALVES, n], F32, name="gate%d" % k)
+            nc.sync.dma_start(gate_sb[:], gate_dram[:, :, s0 : s0 + n])
             gates.append(gate_sb)
 
         windows = [held.tile([P, T], F32, name="window%d" % h) for h in range(HALVES)]
+        x_bf = held.tile([P, PACK, T], BF16, name="x_bf")
+        picked = [held.tile([P, PACK, n], F32, name="picked%d" % i) for i, (s0, n) in enumerate(SLICES)]
+        grouped = [held.tile([P, n, PACK], BF16, name="grouped%d" % i, align_bytes=64) for i, (s0, n) in enumerate(SLICES)]
+        x_code = [held.tile([P, n], U32, name="x_code%d" % i, align_bytes=64) for i, (s0, n) in enumerate(SLICES)]
+        x_scale = [held.tile([P, n], U8, name="x_scale%d" % i, align_bytes=64) for i, (s0, n) in enumerate(SLICES)]
+        acc = [[psum.tile([P, n], F32, name="acc%d_%d" % (k, h)) for h in range(HALVES)] for k, (s0, n) in enumerate(PIECES)]
+        y_sb = [[held.tile([P, n], F32, name="y%d_%d" % (k, h)) for h in range(HALVES)] for k, (s0, n) in enumerate(PIECES)]
 
-        sums = {}
-        for i in range(PIECES):
-            cols = slice(i * PIECE // 16, (i + 1) * PIECE // 16)
-            picked = held.tile([P, PACK, PIECE], F32, name="picked%d" % i)
-            for t in range(PACK):
-                nc.vector.tensor_copy(picked[:, t, :], planes[t][:].indirect(offsets[:, cols]))
-            grouped = held.tile([P, PIECE, PACK], BF16, name="grouped%d" % i, align_bytes=64)
-            nc.scalar.copy(grouped[:], picked[:].rearrange("p t n -> p n t"))
-            x_code = held.tile([P, PIECE], U32, name="x_code%d" % i, align_bytes=64)
-            x_scale = held.tile([P, PIECE], U8, name="x_scale%d" % i, align_bytes=64)
-            nc.vector.quantize_mx(
-                out=x_code[:].bitcast(FP8X4),
-                scales=x_scale[:],
-                in_=grouped[:].rearrange("p n t -> p (n t)"),
-            )
-            for h in range(HALVES):
-                acc = psum.tile([P, PIECE], F32, name="acc%d_%d" % (i, h))
-                for j in range(EXPERTS):
-                    e = i * EXPERTS + j
-                    nc.tensor.matmul_mx(
-                        out=acc[:, j * C : (j + 1) * C],
-                        lhsT=w_code_sb[:, e, h * P : (h + 1) * P].bitcast(FP8X4),
-                        lhsT_scale=w_scale_sb[:, e, h * P : (h + 1) * P],
-                        rhs=x_code[:, j * C : (j + 1) * C].bitcast(FP8X4),
-                        rhs_scale=x_scale[:, j * C : (j + 1) * C],
-                        start=True,
-                        stop=True,
-                    )
-                y_sb = held.tile([P, PIECE], F32, name="y%d_%d" % (i, h))
-                nc.scalar.copy(y_sb[:], acc[:])
-                sums[(i, h)] = y_sb
+        def cols(pair):
+            return slice(pair[0] // 16, (pair[0] + pair[1]) // 16)
 
-        for i in range(PIECES):
-            cols = slice(i * PIECE // 16, (i + 1) * PIECE // 16)
-            for h in range(HALVES):
-                nc.vector.tensor_tensor(
-                    windows[h][:].indirect(offsets[:, cols]),
-                    sums[(i, h)][:],
-                    gates[h][:, i * PIECE : (i + 1) * PIECE],
-                    MULT,
+        def piece_of(slot):
+            return [k for k, (s0, n) in enumerate(PIECES) if s0 <= slot < s0 + n][0]
+
+        def step(word):
+            kind = word[0]
+            a = int(word[1])
+            b = int(word[2]) if len(word) > 2 else 0
+            if kind == "c":
+                nc.scalar.copy(x_bf[:, a, :], planes[a][:])
+            elif kind == "C":
+                nc.gpsimd.tensor_copy(x_bf[:, a, :], planes[a][:])
+            elif kind == "g":
+                nc.vector.tensor_copy(picked[a][:, b, :], planes[b][:].indirect(offsets[:, cols(SLICES[a])]))
+            elif kind == "G":
+                nc.scalar.activation(grouped[a][:, :, b], x_bf[:, b, :].indirect(offsets[:, cols(SLICES[a])]), COPY)
+            elif kind == "i":
+                nc.scalar.copy(grouped[a][:], picked[a][:].rearrange("p t n -> p n t"))
+            elif kind == "v":
+                nc.vector.tensor_copy(grouped[a][:], picked[a][:].rearrange("p t n -> p n t"))
+            elif kind == "b":
+                nc.vector.tensor_copy(grouped[a][:, :, b], planes[b][:].indirect(offsets[:, cols(SLICES[a])]))
+            elif kind == "q":
+                nc.vector.quantize_mx(
+                    out=x_code[a][:].bitcast(FP8X4),
+                    scales=x_scale[a][:],
+                    in_=grouped[a][:].rearrange("p n t -> p (n t)"),
                 )
-        for h in range(HALVES):
-            nc.sync.dma_start(out[h * P : (h + 1) * P, :], windows[h][:])
+            elif kind == "m":
+                s0, n = SLICES[a]
+                for h in range(HALVES):
+                    for j in range(n // C):
+                        e = s0 // C + j
+                        k = piece_of(e * C)
+                        c0 = e * C - PIECES[k][0]
+                        nc.tensor.matmul_mx(
+                            out=acc[k][h][:, c0 : c0 + C],
+                            lhsT=w_code_sb[:, e, h * P : (h + 1) * P].bitcast(FP8X4),
+                            lhsT_scale=w_scale_sb[:, e, h * P : (h + 1) * P],
+                            rhs=x_code[a][:, j * C : (j + 1) * C].bitcast(FP8X4),
+                            rhs_scale=x_scale[a][:, j * C : (j + 1) * C],
+                            start=True,
+                            stop=True,
+                        )
+            elif kind == "y":
+                nc.scalar.copy(y_sb[a][b][:], acc[a][b][:])
+            elif kind == "s":
+                nc.vector.tensor_tensor(windows[b][:].indirect(offsets[:, cols(PIECES[a])]), y_sb[a][b][:], gates[a][:, b, :], MULT)
+            elif kind == "o":
+                nc.sync.dma_start(out[a * P : (a + 1) * P, :], windows[a][:])
+
+        for word in ORDER.split():
+            step(word)

@@ -21,7 +21,7 @@ HALVES = N // P
 
 SLICES = [(0, 256), (256, 256), (512, 256), (768, 256)]
 PIECES = [(0, 256), (256, 256), (512, 512)]
-ORDER = """c0 c1 c2 c3 g00 g10 g01 g11 g02 g12 g03 v0 g13 q0 m0 y00 y01 v1 q1 m1 y10 y11
+ORDER = """C0 C1 C2 C3 g00 g10 g01 g11 g02 g12 g03 v0 g13 q0 m0 y00 y01 v1 q1 m1 y10 y11
 G20 G21 G22 G23 q2 m2 G30 G31 G32 G33 q3 m3 y20 y21 s00 s01 s10 s11 s20 o0 s21 o1"""
 
 

@@ -21,7 +21,7 @@ HALVES = N // P
 
 SLICES = [(0, 256), (256, 256), (512, 256), (768, 256)]
 PIECES = [(0, 256), (256, 256), (512, 512)]
-ORDER = """C0 C1 C2 C3 g00 g10 g01 g11 g02 g12 g03 v0 g13 q0 m0 y00 y01 v1 q1 m1 y10 y11
+ORDER = """C0 C1 C2 C3 b00 b10 b01 b11 b02 b12 b03 b13 q0 m0 y00 y01 q1 m1 y10 y11
 G20 G21 G22 G23 q2 m2 G30 G31 G32 G33 q3 m3 y20 y21 s00 s01 s10 s11 s20 o0 s21 o1"""
 
 
@@ -36,11 +36,11 @@ def tile_routed_moe_kernel(tc, xT, w_words, w_scales, gate, offs, out):
         nc.sync.dma_start(offsets[:], offs)
 
         x_rows = xT.rearrange("(g p t) n -> g p t n", p=P, t=PACK)
+        raw = held.tile([P, PACK, T], F32, name="raw")
         planes = []
         for t in range(PACK):
-            plane = held.tile([P, T], F32, name="plane%d" % t)
-            nc.sync.dma_start(plane[:], x_rows[0, :, t, :])
-            planes.append(plane)
+            nc.sync.dma_start(raw[:, t, :], x_rows[0, :, t, :])
+            planes.append(raw[:, t, :])
 
         w_scale_sb = held.tile([P, E, N], U8, name="w_scale_sb", align_bytes=64)
         nc.vector.memset(w_scale_sb[:].rearrange("p e n -> p (e n)").bitcast(I32), 0)
@@ -79,11 +79,11 @@ def tile_routed_moe_kernel(tc, xT, w_words, w_scales, gate, offs, out):
             a = int(word[1])
             b = int(word[2]) if len(word) > 2 else 0
             if kind == "c":
-                nc.scalar.copy(x_bf[:, a, :], planes[a][:])
+                nc.scalar.copy(x_bf[:, a, :], planes[a])
             elif kind == "C":
-                nc.gpsimd.tensor_copy(x_bf[:, a, :], planes[a][:])
+                nc.gpsimd.tensor_copy(x_bf[:, a, :], planes[a])
             elif kind == "g":
-                nc.vector.tensor_copy(picked[a][:, b, :], planes[b][:].indirect(offsets[:, cols(SLICES[a])]))
+                nc.vector.tensor_copy(picked[a][:, b, :], planes[b].indirect(offsets[:, cols(SLICES[a])]))
             elif kind == "G":
                 nc.scalar.activation(grouped[a][:, :, b], x_bf[:, b, :].indirect(offsets[:, cols(SLICES[a])]), COPY)
             elif kind == "i":
@@ -91,7 +91,7 @@ def tile_routed_moe_kernel(tc, xT, w_words, w_scales, gate, offs, out):
             elif kind == "v":
                 nc.vector.tensor_copy(grouped[a][:], picked[a][:].rearrange("p t n -> p n t"))
             elif kind == "b":
-                nc.vector.tensor_copy(grouped[a][:, :, b], planes[b][:].indirect(offsets[:, cols(SLICES[a])]))
+                nc.vector.tensor_copy(grouped[a][:, :, b], planes[b].indirect(offsets[:, cols(SLICES[a])]))
             elif kind == "q":
                 nc.vector.quantize_mx(
                     out=x_code[a][:].bitcast(FP8X4),

@@ -12,17 +12,21 @@ I32 = mybir.dt.int32
 U16 = mybir.dt.uint16
 U8 = mybir.dt.uint8
 FP8X4 = mybir.dt.float8_e4m3fn_x4
-MULT = mybir.AluOpType.mult
-COPY = mybir.ActivationFunctionType.Copy
 
 P = 128
 PACK = 4
-HALVES = N // P
+QUADRANT = 32
+SCALE_ROWS = QUADRANT // 8
+MX_ALIGN = 64
+SLOTS = E * C
+FEATURE_BLOCKS = N // P
+PER_COLUMN = 16
 
-SLICES = [(0, 256), (256, 256), (512, 256), (768, 256)]
-PIECES = [(0, 256), (256, 256), (512, 512)]
-ORDER = """C0 C1 C2 C3 b00 b10 b01 b11 b02 b12 b03 b13 q0 m0 y00 y01 q1 m1 y10 y11
-G20 G21 G22 G23 q2 m2 G30 G31 G32 G33 q3 m3 y20 y21 s00 s01 s10 s11 s20 o0 s21 o1"""
+SLICE = 2 * C
+SLICES = SLOTS // SLICE
+VECTOR_SLICES = (0, 1)
+SCALAR_SLICES = (2, 3)
+PIECES = ((0,), (1,), (2, 3))
 
 
 def tile_routed_moe_kernel(tc, xT, w_words, w_scales, gate, offs, out):
@@ -32,94 +36,104 @@ def tile_routed_moe_kernel(tc, xT, w_words, w_scales, gate, offs, out):
         held = ctx.enter_context(tc.tile_pool(name="held", bufs=1))
         psum = ctx.enter_context(tc.psum_pool(name="psum", bufs=1))
 
-        offsets = lists.tile([P, E * C // 16], U16, name="offsets")
+        def list_columns(first_slice, count):
+            per_slice = SLICE // PER_COLUMN
+            return slice(first_slice * per_slice, (first_slice + count) * per_slice)
+
+        offsets = lists.tile([P, SLOTS // PER_COLUMN], U16, name="offsets")
         nc.sync.dma_start(offsets[:], offs)
 
-        x_rows = xT.rearrange("(g p t) n -> g p t n", p=P, t=PACK)
-        raw = held.tile([P, PACK, T], F32, name="raw")
-        planes = []
+        x_f32 = held.tile([P, PACK, T], F32, name="x_f32")
+        x_planes = xT.rearrange("(p t) m -> p t m", t=PACK)
         for t in range(PACK):
-            nc.sync.dma_start(raw[:, t, :], x_rows[0, :, t, :])
-            planes.append(raw[:, t, :])
+            nc.sync.dma_start(x_f32[:, t, :], x_planes[:, t, :])
 
-        w_scale_sb = held.tile([P, E, N], U8, name="w_scale_sb", align_bytes=64)
-        nc.vector.memset(w_scale_sb[:].rearrange("p e n -> p (e n)").bitcast(I32), 0)
-        w_code_sb = held.tile([P, E, N], U32, name="w_code_sb", align_bytes=64)
-        w_code_dram = w_words.rearrange("e a p n r -> p (e a) (n r)").bitcast(I32)
-        gate_dram = gate.rearrange("(h p) j -> p h j", p=P)
-        gates = []
-        for k, (s0, n) in enumerate(PIECES):
-            for q in range(4):
+        w_code = held.tile([P, E, N], U32, name="w_code", align_bytes=MX_ALIGN)
+        w_scale = held.tile([P, E, N], U8, name="w_scale", align_bytes=MX_ALIGN)
+        nc.vector.memset(w_scale[:].rearrange("p e n -> p (e n)").bitcast(I32), 0)
+        w_words_by_partition = w_words.rearrange("e a p n r -> p (e a) (n r)").bitcast(I32)
+        gate_by_partition = gate.rearrange("(h p) j -> p h j", p=P)
+        gate_sb = []
+        for piece in PIECES:
+            experts = slice(piece[0] * SLICE // C, (piece[-1] + 1) * SLICE // C)
+            for quadrant in range(P // QUADRANT):
                 nc.sync.dma_start(
-                    w_scale_sb[32 * q : 32 * q + 4, s0 // C : (s0 + n) // C, :].bitcast(I32),
-                    w_scales[s0 // C : (s0 + n) // C, 0, 4 * q : 4 * q + 4, :].rearrange("e r n -> r e n").bitcast(I32),
+                    w_scale[QUADRANT * quadrant : QUADRANT * quadrant + SCALE_ROWS, experts, :].bitcast(I32),
+                    w_scales[experts, 0, SCALE_ROWS * quadrant : SCALE_ROWS * (quadrant + 1), :].rearrange("e q n -> q e n").bitcast(I32),
                 )
-            nc.sync.dma_start(w_code_sb[:, s0 // C : (s0 + n) // C, :].bitcast(I32), w_code_dram[:, s0 // C : (s0 + n) // C, :])
-            gate_sb = held.tile([P, HALVES, n], F32, name="gate%d" % k)
-            nc.sync.dma_start(gate_sb[:], gate_dram[:, :, s0 : s0 + n])
-            gates.append(gate_sb)
+            nc.sync.dma_start(w_code[:, experts, :].bitcast(I32), w_words_by_partition[:, experts, :])
+            piece_gate = held.tile([P, FEATURE_BLOCKS, len(piece) * SLICE], F32, name="gate%d" % piece[0])
+            nc.sync.dma_start(piece_gate[:], gate_by_partition[:, :, piece[0] * SLICE : (piece[-1] + 1) * SLICE])
+            gate_sb.append(piece_gate)
 
-        windows = [held.tile([P, T], F32, name="window%d" % h) for h in range(HALVES)]
-        x_bf = held.tile([P, PACK, T], BF16, name="x_bf")
-        picked = [held.tile([P, PACK, n], F32, name="picked%d" % i) for i, (s0, n) in enumerate(SLICES)]
-        grouped = [held.tile([P, n, PACK], BF16, name="grouped%d" % i, align_bytes=64) for i, (s0, n) in enumerate(SLICES)]
-        x_code = [held.tile([P, n], U32, name="x_code%d" % i, align_bytes=64) for i, (s0, n) in enumerate(SLICES)]
-        x_scale = [held.tile([P, n], U8, name="x_scale%d" % i, align_bytes=64) for i, (s0, n) in enumerate(SLICES)]
-        acc = [[psum.tile([P, n], F32, name="acc%d_%d" % (k, h)) for h in range(HALVES)] for k, (s0, n) in enumerate(PIECES)]
-        y_sb = [[held.tile([P, n], F32, name="y%d_%d" % (k, h)) for h in range(HALVES)] for k, (s0, n) in enumerate(PIECES)]
+        x_bf16 = held.tile([P, PACK, T], BF16, name="x_bf16")
+        nc.vector.tensor_copy(x_bf16[:, 0, :], x_f32[:, 0, :])
+        for t in range(1, PACK):
+            nc.gpsimd.tensor_copy(x_bf16[:, t, :], x_f32[:, t, :])
 
-        def cols(pair):
-            return slice(pair[0] // 16, (pair[0] + pair[1]) // 16)
+        grouped = [held.tile([P, SLICE, PACK], BF16, name="grouped%d" % i, align_bytes=MX_ALIGN) for i in range(SLICES)]
+        x_code = [held.tile([P, SLICE], U32, name="x_code%d" % i, align_bytes=MX_ALIGN) for i in range(SLICES)]
+        x_scale = [held.tile([P, SLICE], U8, name="x_scale%d" % i, align_bytes=MX_ALIGN) for i in range(SLICES)]
+        sums = [
+            [psum.tile([P, len(piece) * SLICE], F32, name="sums%d_%d" % (piece[0], h)) for h in range(FEATURE_BLOCKS)]
+            for piece in PIECES
+        ]
+        sums_sb = [
+            [held.tile([P, len(piece) * SLICE], F32, name="sums_sb%d_%d" % (piece[0], h)) for h in range(FEATURE_BLOCKS)]
+            for piece in PIECES
+        ]
 
-        def piece_of(slot):
-            return [k for k, (s0, n) in enumerate(PIECES) if s0 <= slot < s0 + n][0]
+        def quantize_and_multiply(i):
+            nc.vector.quantize_mx(
+                out=x_code[i][:].bitcast(FP8X4),
+                scales=x_scale[i][:],
+                in_=grouped[i][:].rearrange("p j t -> p (j t)"),
+            )
+            number = [i in piece for piece in PIECES].index(True)
+            for h in range(FEATURE_BLOCKS):
+                for e in range(i * SLICE // C, (i + 1) * SLICE // C):
+                    features = slice(h * P, (h + 1) * P)
+                    in_slice = e * C - i * SLICE
+                    in_piece = e * C - PIECES[number][0] * SLICE
+                    nc.tensor.matmul_mx(
+                        out=sums[number][h][:, in_piece : in_piece + C],
+                        lhsT=w_code[:, e, features].bitcast(FP8X4),
+                        lhsT_scale=w_scale[:, e, features],
+                        rhs=x_code[i][:, in_slice : in_slice + C].bitcast(FP8X4),
+                        rhs_scale=x_scale[i][:, in_slice : in_slice + C],
+                        start=True,
+                        stop=True,
+                    )
 
-        def step(word):
-            kind = word[0]
-            a = int(word[1])
-            b = int(word[2]) if len(word) > 2 else 0
-            if kind == "c":
-                nc.scalar.copy(x_bf[:, a, :], planes[a])
-            elif kind == "C":
-                nc.gpsimd.tensor_copy(x_bf[:, a, :], planes[a])
-            elif kind == "g":
-                nc.vector.tensor_copy(picked[a][:, b, :], planes[b].indirect(offsets[:, cols(SLICES[a])]))
-            elif kind == "G":
-                nc.scalar.activation(grouped[a][:, :, b], x_bf[:, b, :].indirect(offsets[:, cols(SLICES[a])]), COPY)
-            elif kind == "i":
-                nc.scalar.copy(grouped[a][:], picked[a][:].rearrange("p t n -> p n t"))
-            elif kind == "v":
-                nc.vector.tensor_copy(grouped[a][:], picked[a][:].rearrange("p t n -> p n t"))
-            elif kind == "b":
-                nc.vector.tensor_copy(grouped[a][:, :, b], planes[b].indirect(offsets[:, cols(SLICES[a])]))
-            elif kind == "q":
-                nc.vector.quantize_mx(
-                    out=x_code[a][:].bitcast(FP8X4),
-                    scales=x_scale[a][:],
-                    in_=grouped[a][:].rearrange("p n t -> p (n t)"),
+        def copy_sums(number):
+            for h in range(FEATURE_BLOCKS):
+                nc.scalar.copy(sums_sb[number][h][:], sums[number][h][:])
+
+        for t in range(PACK):
+            for i in VECTOR_SLICES:
+                nc.vector.tensor_copy(grouped[i][:, :, t], x_f32[:, t, :].indirect(offsets[:, list_columns(i, 1)]))
+        for i in VECTOR_SLICES:
+            quantize_and_multiply(i)
+            copy_sums(i)
+
+        for i in SCALAR_SLICES:
+            for t in range(PACK):
+                nc.scalar.activation(
+                    grouped[i][:, :, t],
+                    x_bf16[:, t, :].indirect(offsets[:, list_columns(i, 1)]),
+                    mybir.ActivationFunctionType.Copy,
                 )
-            elif kind == "m":
-                s0, n = SLICES[a]
-                for h in range(HALVES):
-                    for j in range(n // C):
-                        e = s0 // C + j
-                        k = piece_of(e * C)
-                        c0 = e * C - PIECES[k][0]
-                        nc.tensor.matmul_mx(
-                            out=acc[k][h][:, c0 : c0 + C],
-                            lhsT=w_code_sb[:, e, h * P : (h + 1) * P].bitcast(FP8X4),
-                            lhsT_scale=w_scale_sb[:, e, h * P : (h + 1) * P],
-                            rhs=x_code[a][:, j * C : (j + 1) * C].bitcast(FP8X4),
-                            rhs_scale=x_scale[a][:, j * C : (j + 1) * C],
-                            start=True,
-                            stop=True,
-                        )
-            elif kind == "y":
-                nc.scalar.copy(y_sb[a][b][:], acc[a][b][:])
-            elif kind == "s":
-                nc.vector.tensor_tensor(windows[b][:].indirect(offsets[:, cols(PIECES[a])]), y_sb[a][b][:], gates[a][:, b, :], MULT)
-            elif kind == "o":
-                nc.sync.dma_start(out[a * P : (a + 1) * P, :], windows[a][:])
+            quantize_and_multiply(i)
+        copy_sums(len(PIECES) - 1)
 
-        for word in ORDER.split():
-            step(word)
+        windows = [held.tile([P, T], F32, name="window%d" % h) for h in range(FEATURE_BLOCKS)]
+        for number, piece in enumerate(PIECES):
+            for h in range(FEATURE_BLOCKS):
+                nc.vector.tensor_tensor(
+                    windows[h][:].indirect(offsets[:, list_columns(piece[0], len(piece))]),
+                    sums_sb[number][h][:],
+                    gate_sb[number][:, h, :],
+                    mybir.AluOpType.mult,
+                )
+                if number == len(PIECES) - 1:
+                    nc.sync.dma_start(out[h * P : (h + 1) * P, :], windows[h][:])

@@ -24,9 +24,7 @@ PER_COLUMN = 16
 
 SLICE = 2 * C
 SLICES = SLOTS // SLICE
-VECTOR_SLICES = (0, 1)
-SCALAR_SLICES = (2, 3)
-PIECES = ((0,), (1,), (2, 3))
+LOAD_GROUPS = ((0,), (1,), (2, 3))
 
 
 def tile_routed_moe_kernel(tc, xT, w_words, w_scales, gate, offs, out):
@@ -36,9 +34,9 @@ def tile_routed_moe_kernel(tc, xT, w_words, w_scales, gate, offs, out):
         held = ctx.enter_context(tc.tile_pool(name="held", bufs=1))
         psum = ctx.enter_context(tc.psum_pool(name="psum", bufs=1))
 
-        def list_columns(first_slice, count):
+        def list_columns(i):
             per_slice = SLICE // PER_COLUMN
-            return slice(first_slice * per_slice, (first_slice + count) * per_slice)
+            return slice(i * per_slice, (i + 1) * per_slice)
 
         offsets = lists.tile([P, SLOTS // PER_COLUMN], U16, name="offsets")
         nc.sync.dma_start(offsets[:], offs)
@@ -53,35 +51,40 @@ def tile_routed_moe_kernel(tc, xT, w_words, w_scales, gate, offs, out):
         nc.vector.memset(w_scale[:].rearrange("p e n -> p (e n)").bitcast(I32), 0)
         w_words_by_partition = w_words.rearrange("e a p n r -> p (e a) (n r)").bitcast(I32)
         gate_by_partition = gate.rearrange("(h p) j -> p h j", p=P)
-        gate_sb = []
-        for piece in PIECES:
-            experts = slice(piece[0] * SLICE // C, (piece[-1] + 1) * SLICE // C)
-            for quadrant in range(P // QUADRANT):
-                nc.sync.dma_start(
-                    w_scale[QUADRANT * quadrant : QUADRANT * quadrant + SCALE_ROWS, experts, :].bitcast(I32),
-                    w_scales[experts, 0, SCALE_ROWS * quadrant : SCALE_ROWS * (quadrant + 1), :].rearrange("e q n -> q e n").bitcast(I32),
-                )
+        gate_of_slice = {}
+        for quadrant in range(P // QUADRANT):
+            nc.sync.dma_start(
+                w_scale[QUADRANT * quadrant : QUADRANT * quadrant + SCALE_ROWS, :, :].bitcast(I32),
+                w_scales[:, 0, SCALE_ROWS * quadrant : SCALE_ROWS * (quadrant + 1), :].rearrange("e q n -> q e n").bitcast(I32),
+            )
+        for group in LOAD_GROUPS:
+            experts = slice(group[0] * SLICE // C, (group[-1] + 1) * SLICE // C)
             nc.sync.dma_start(w_code[:, experts, :].bitcast(I32), w_words_by_partition[:, experts, :])
-            piece_gate = held.tile([P, FEATURE_BLOCKS, len(piece) * SLICE], F32, name="gate%d" % piece[0])
-            nc.sync.dma_start(piece_gate[:], gate_by_partition[:, :, piece[0] * SLICE : (piece[-1] + 1) * SLICE])
-            gate_sb.append(piece_gate)
+            group_gate = held.tile([P, FEATURE_BLOCKS, len(group) * SLICE], F32, name="gate%d" % group[0])
+            nc.sync.dma_start(group_gate[:], gate_by_partition[:, :, group[0] * SLICE : (group[-1] + 1) * SLICE])
+            for place, i in enumerate(group):
+                gate_of_slice[i] = group_gate[:, :, place * SLICE : (place + 1) * SLICE]
 
         x_bf16 = held.tile([P, PACK, T], BF16, name="x_bf16")
-        nc.vector.tensor_copy(x_bf16[:, 0, :], x_f32[:, 0, :])
-        for t in range(1, PACK):
+        for t in range(PACK):
             nc.gpsimd.tensor_copy(x_bf16[:, t, :], x_f32[:, t, :])
 
-        grouped = [held.tile([P, SLICE, PACK], BF16, name="grouped%d" % i, align_bytes=MX_ALIGN) for i in range(SLICES)]
-        x_code = [held.tile([P, SLICE], U32, name="x_code%d" % i, align_bytes=MX_ALIGN) for i in range(SLICES)]
+        grouped = {}
+        sums_sb = {}
+        x_code = {}
         x_scale = [held.tile([P, SLICE], U8, name="x_scale%d" % i, align_bytes=MX_ALIGN) for i in range(SLICES)]
-        sums = [
-            [psum.tile([P, len(piece) * SLICE], F32, name="sums%d_%d" % (piece[0], h)) for h in range(FEATURE_BLOCKS)]
-            for piece in PIECES
-        ]
-        sums_sb = [
-            [held.tile([P, len(piece) * SLICE], F32, name="sums_sb%d_%d" % (piece[0], h)) for h in range(FEATURE_BLOCKS)]
-            for piece in PIECES
-        ]
+        sums = [[psum.tile([P, SLICE], F32, name="sums%d_%d" % (i, h)) for h in range(FEATURE_BLOCKS)] for i in range(SLICES)]
+        windows = [held.tile([P, T], F32, name="window%d" % h) for h in range(FEATURE_BLOCKS)]
+
+        def vector_gather(i, t):
+            nc.vector.tensor_copy(grouped[i][:, :, t], x_f32[:, t, :].indirect(offsets[:, list_columns(i)]))
+
+        def scalar_gather(i, t):
+            nc.scalar.activation(
+                grouped[i][:, :, t],
+                x_bf16[:, t, :].indirect(offsets[:, list_columns(i)]),
+                mybir.ActivationFunctionType.Copy,
+            )
 
         def quantize_and_multiply(i):
             nc.vector.quantize_mx(
@@ -89,14 +92,12 @@ def tile_routed_moe_kernel(tc, xT, w_words, w_scales, gate, offs, out):
                 scales=x_scale[i][:],
                 in_=grouped[i][:].rearrange("p j t -> p (j t)"),
             )
-            number = [i in piece for piece in PIECES].index(True)
             for h in range(FEATURE_BLOCKS):
                 for e in range(i * SLICE // C, (i + 1) * SLICE // C):
                     features = slice(h * P, (h + 1) * P)
                     in_slice = e * C - i * SLICE
-                    in_piece = e * C - PIECES[number][0] * SLICE
                     nc.tensor.matmul_mx(
-                        out=sums[number][h][:, in_piece : in_piece + C],
+                        out=sums[i][h][:, in_slice : in_slice + C],
                         lhsT=w_code[:, e, features].bitcast(FP8X4),
                         lhsT_scale=w_scale[:, e, features],
                         rhs=x_code[i][:, in_slice : in_slice + C].bitcast(FP8X4),
@@ -105,35 +106,63 @@ def tile_routed_moe_kernel(tc, xT, w_words, w_scales, gate, offs, out):
                         stop=True,
                     )
 
-        def copy_sums(number):
-            for h in range(FEATURE_BLOCKS):
-                nc.scalar.copy(sums_sb[number][h][:], sums[number][h][:])
+        def copy_sums(i, h):
+            nc.scalar.copy(sums_sb[i, h][:], sums[i][h][:])
 
+        def scatter(i, h):
+            nc.vector.tensor_tensor(
+                windows[h][:].indirect(offsets[:, list_columns(i)]),
+                sums_sb[i, h][:],
+                gate_of_slice[i][:, h, :],
+                mybir.AluOpType.mult,
+            )
+
+        for i in range(3):
+            grouped[i] = held.tile([P, SLICE, PACK], BF16, name="grouped%d" % i, align_bytes=MX_ALIGN)
+        x_code[0] = held.tile([P, SLICE], U32, name="x_code0", align_bytes=MX_ALIGN)
+        x_code[1] = held.tile([P, SLICE], U32, name="x_code1", tag="slot_a", align_bytes=MX_ALIGN)
+        for i in range(SLICES):
+            for h in range(FEATURE_BLOCKS):
+                if h == 0 and i < 2:
+                    sums_sb[i, h] = held.tile([P, SLICE], F32, name="sums_sb%d_%d" % (i, h), tag="slot_%d" % i, align_bytes=MX_ALIGN)
+                else:
+                    sums_sb[i, h] = held.tile([P, SLICE], F32, name="sums_sb%d_%d" % (i, h))
+
+        vector_gather(0, 0)
+        scalar_gather(1, 0)
+        scalar_gather(2, 0)
+        vector_gather(0, 1)
+        scalar_gather(1, 1)
+        scalar_gather(2, 1)
+        vector_gather(0, 2)
+        vector_gather(1, 2)
+        scalar_gather(2, 2)
+        vector_gather(0, 3)
+        quantize_and_multiply(0)
+        nc.vector.tensor_copy(sums_sb[0, 0][:], sums[0][0][:])
+        copy_sums(0, 1)
+        vector_gather(1, 3)
+        quantize_and_multiply(1)
+        copy_sums(1, 0)
+        copy_sums(1, 1)
+        scatter(0, 0)
+        scatter(0, 1)
+        scalar_gather(2, 3)
+        x_code[2] = held.tile([P, SLICE], U32, name="x_code2", tag="slot_0", align_bytes=MX_ALIGN)
+        quantize_and_multiply(2)
+        copy_sums(2, 0)
+        copy_sums(2, 1)
+        grouped[3] = held.tile([P, SLICE, PACK], BF16, name="grouped3", tag="slot_a", align_bytes=MX_ALIGN)
         for t in range(PACK):
-            for i in VECTOR_SLICES:
-                nc.vector.tensor_copy(grouped[i][:, :, t], x_f32[:, t, :].indirect(offsets[:, list_columns(i, 1)]))
-        for i in VECTOR_SLICES:
-            quantize_and_multiply(i)
-            copy_sums(i)
-
-        for i in SCALAR_SLICES:
-            for t in range(PACK):
-                nc.scalar.activation(
-                    grouped[i][:, :, t],
-                    x_bf16[:, t, :].indirect(offsets[:, list_columns(i, 1)]),
-                    mybir.ActivationFunctionType.Copy,
-                )
-            quantize_and_multiply(i)
-        copy_sums(len(PIECES) - 1)
-
-        windows = [held.tile([P, T], F32, name="window%d" % h) for h in range(FEATURE_BLOCKS)]
-        for number, piece in enumerate(PIECES):
+            scalar_gather(3, t)
+        scatter(1, 0)
+        scatter(1, 1)
+        x_code[3] = held.tile([P, SLICE], U32, name="x_code3", tag="slot_1", align_bytes=MX_ALIGN)
+        quantize_and_multiply(3)
+        copy_sums(3, 0)
+        copy_sums(3, 1)
+        for i in (2, 3):
             for h in range(FEATURE_BLOCKS):
-                nc.vector.tensor_tensor(
-                    windows[h][:].indirect(offsets[:, list_columns(piece[0], len(piece))]),
-                    sums_sb[number][h][:],
-                    gate_sb[number][:, h, :],
-                    mybir.AluOpType.mult,
-                )
-                if number == len(PIECES) - 1:
-                    nc.sync.dma_start(out[h * P : (h + 1) * P, :], windows[h][:])
+                scatter(i, h)
+        for h in range(FEATURE_BLOCKS):
+            nc.sync.dma_start(out[h * P : (h + 1) * P, :], windows[h][:])

@@ -57,16 +57,29 @@ def tile_routed_moe_kernel(tc, xT, w_words, w_scales, gate, offs, out):
                 w_scale[QUADRANT * quadrant : QUADRANT * quadrant + SCALE_ROWS, :, :].bitcast(I32),
                 w_scales[:, 0, SCALE_ROWS * quadrant : SCALE_ROWS * (quadrant + 1), :].rearrange("e q n -> q e n").bitcast(I32),
             )
-        for group in LOAD_GROUPS:
-            experts = slice(group[0] * SLICE // C, (group[-1] + 1) * SLICE // C)
-            nc.sync.dma_start(w_code[:, experts, :].bitcast(I32), w_words_by_partition[:, experts, :])
-            group_gate = held.tile([P, FEATURE_BLOCKS, len(group) * SLICE], F32, name="gate%d" % group[0])
-            nc.sync.dma_start(group_gate[:], gate_by_partition[:, :, group[0] * SLICE : (group[-1] + 1) * SLICE])
-            for place, i in enumerate(group):
-                gate_of_slice[i] = group_gate[:, :, place * SLICE : (place + 1) * SLICE]
+        def load_codes(first, count, features=slice(0, N)):
+            experts = slice(first * SLICE // C, (first + count) * SLICE // C)
+            nc.sync.dma_start(w_code[:, experts, features].bitcast(I32), w_words_by_partition[:, experts, features])
+
+        def load_gate(first, count, blocks):
+            tile = held.tile([P, len(blocks), count * SLICE], F32, name="gate%d_%d" % (first, blocks[0]), tag="gate%d_%d" % (first, blocks[0]), align_bytes=MX_ALIGN)
+            nc.sync.dma_start(tile[:], gate_by_partition[:, blocks[0] : blocks[-1] + 1, first * SLICE : (first + count) * SLICE])
+            for place in range(count):
+                for k, h in enumerate(blocks):
+                    gate_of_slice[first + place, h] = tile[:, k, place * SLICE : (place + 1) * SLICE]
+
+        load_codes(0, 1, slice(0, P))
+        load_gate(0, 1, (0,))
+        load_codes(0, 1, slice(P, N))
+        load_gate(0, 1, (1,))
+        load_codes(1, 1)
+        load_gate(1, 1, (0, 1))
+        load_codes(2, 2)
+        load_gate(2, 2, (0, 1))
 
         x_bf16 = held.tile([P, PACK, T], BF16, name="x_bf16")
-        for t in range(PACK):
+        nc.vector.tensor_copy(x_bf16[:, 0, :], x_f32[:, 0, :])
+        for t in range(1, PACK):
             nc.gpsimd.tensor_copy(x_bf16[:, t, :], x_f32[:, t, :])
 
         grouped = {}
@@ -113,48 +126,52 @@ def tile_routed_moe_kernel(tc, xT, w_words, w_scales, gate, offs, out):
             nc.vector.tensor_tensor(
                 windows[h][:].indirect(offsets[:, list_columns(i)]),
                 sums_sb[i, h][:],
-                gate_of_slice[i][:, h, :],
+                gate_of_slice[i, h],
+                mybir.AluOpType.mult,
+            )
+
+        def first_scatter(e):
+            per_expert = C // PER_COLUMN
+            nc.vector.tensor_tensor(
+                windows[0][:].indirect(offsets[:, e * per_expert : (e + 1) * per_expert]),
+                first_sums[e][:],
+                gate_of_slice[0, 0][:, e * C : (e + 1) * C],
                 mybir.AluOpType.mult,
             )
 
         for i in range(3):
             grouped[i] = held.tile([P, SLICE, PACK], BF16, name="grouped%d" % i, align_bytes=MX_ALIGN)
         x_code[0] = held.tile([P, SLICE], U32, name="x_code0", align_bytes=MX_ALIGN)
-        x_code[1] = held.tile([P, SLICE], U32, name="x_code1", tag="slot_a", align_bytes=MX_ALIGN)
-        for i in range(SLICES):
+        first_sums = [held.tile([P, C], F32, name="first_sums%d" % e, tag="slot_f%d" % e, align_bytes=MX_ALIGN) for e in range(2)]
+        sums_sb[0, 1] = held.tile([P, SLICE], F32, name="sums_sb0_1")
+        sums_sb[1, 0] = held.tile([P, SLICE], F32, name="sums_sb1_0", tag="slot_1", align_bytes=MX_ALIGN)
+        sums_sb[1, 1] = held.tile([P, SLICE], F32, name="sums_sb1_1")
+        for i in (2, 3):
             for h in range(FEATURE_BLOCKS):
-                if h == 0 and i < 2:
-                    sums_sb[i, h] = held.tile([P, SLICE], F32, name="sums_sb%d_%d" % (i, h), tag="slot_%d" % i, align_bytes=MX_ALIGN)
-                else:
-                    sums_sb[i, h] = held.tile([P, SLICE], F32, name="sums_sb%d_%d" % (i, h))
+                sums_sb[i, h] = held.tile([P, SLICE], F32, name="sums_sb%d_%d" % (i, h))
 
-        vector_gather(0, 0)
-        scalar_gather(1, 0)
-        scalar_gather(2, 0)
-        vector_gather(0, 1)
-        scalar_gather(1, 1)
-        scalar_gather(2, 1)
-        vector_gather(0, 2)
-        vector_gather(1, 2)
-        scalar_gather(2, 2)
-        vector_gather(0, 3)
+        for t in range(PACK):
+            vector_gather(0, t)
+            scalar_gather(1, t)
+            scalar_gather(2, t)
         quantize_and_multiply(0)
-        nc.vector.tensor_copy(sums_sb[0, 0][:], sums[0][0][:])
+        for e in range(2):
+            nc.vector.tensor_copy(first_sums[e][:], sums[0][0][:, e * C : (e + 1) * C])
         copy_sums(0, 1)
-        vector_gather(1, 3)
+        for e in range(2):
+            first_scatter(e)
+        x_code[1] = held.tile([P, SLICE], U32, name="x_code1", tag="slot_f0", align_bytes=MX_ALIGN)
         quantize_and_multiply(1)
+        x_code[2] = held.tile([P, SLICE], U32, name="x_code2", tag="slot_f1", align_bytes=MX_ALIGN)
+        quantize_and_multiply(2)
+        scatter(0, 1)
         copy_sums(1, 0)
         copy_sums(1, 1)
-        scatter(0, 0)
-        scatter(0, 1)
-        scalar_gather(2, 3)
-        x_code[2] = held.tile([P, SLICE], U32, name="x_code2", tag="slot_0", align_bytes=MX_ALIGN)
-        quantize_and_multiply(2)
-        copy_sums(2, 0)
-        copy_sums(2, 1)
-        grouped[3] = held.tile([P, SLICE, PACK], BF16, name="grouped3", tag="slot_a", align_bytes=MX_ALIGN)
+        grouped[3] = held.tile([P, SLICE, PACK], BF16, name="grouped3", tag="slot_f0", align_bytes=MX_ALIGN)
         for t in range(PACK):
             scalar_gather(3, t)
+        copy_sums(2, 0)
+        copy_sums(2, 1)
         scatter(1, 0)
         scatter(1, 1)
         x_code[3] = held.tile([P, SLICE], U32, name="x_code3", tag="slot_1", align_bytes=MX_ALIGN)

@@ -77,6 +77,10 @@ def tile_routed_moe_kernel(tc, xT, w_words, w_scales, gate, offs, out):
         load_codes(2, 2)
         load_gate(2, 2, (0, 1))
 
+        warm = held.tile([P, 2], F32, name="warm")
+        nc.gpsimd.memset(warm[:, 0:1], 0.0)
+        nc.scalar.activation(warm[:, 1:2], warm[:, 0:1], mybir.ActivationFunctionType.Copy)
+
         x_bf16 = held.tile([P, PACK, T], BF16, name="x_bf16")
         nc.vector.tensor_copy(x_bf16[:, 0, :], x_f32[:, 0, :])
         for t in range(1, PACK):
@@ -86,11 +90,30 @@ def tile_routed_moe_kernel(tc, xT, w_words, w_scales, gate, offs, out):
         sums_sb = {}
         x_code = {}
         x_scale = [held.tile([P, SLICE], U8, name="x_scale%d" % i, align_bytes=MX_ALIGN) for i in range(SLICES)]
-        sums = [[psum.tile([P, SLICE], F32, name="sums%d_%d" % (i, h)) for h in range(FEATURE_BLOCKS)] for i in range(SLICES)]
         windows = [held.tile([P, T], F32, name="window%d" % h) for h in range(FEATURE_BLOCKS)]
 
-        def vector_gather(i, t):
-            nc.vector.tensor_copy(grouped[i][:, :, t], x_f32[:, t, :].indirect(offsets[:, list_columns(i)]))
+        bank_of = {}
+        first_bank = [psum.tile([P, C], F32, name="first_bank%d" % e) for e in range(2)]
+        sums = {}
+        sums[0, 1] = psum.tile([P, SLICE], F32, name="sums0_1")
+        for i in (1, 2):
+            for h in range(FEATURE_BLOCKS):
+                sums[i, h] = psum.tile([P, SLICE], F32, name="sums%d_%d" % (i, h))
+        last_bank = psum.tile([P, FEATURE_BLOCKS, SLICE], F32, name="last_bank")
+        for e in range(E):
+            i = e * C // SLICE
+            in_slice = e * C - i * SLICE
+            for h in range(FEATURE_BLOCKS):
+                if i == 0 and h == 0:
+                    bank_of[e, h] = first_bank[e][:]
+                elif i == SLICES - 1:
+                    bank_of[e, h] = last_bank[:, h, in_slice : in_slice + C]
+                else:
+                    bank_of[e, h] = sums[i, h][:, in_slice : in_slice + C]
+
+        def vector_gather(i, t, first=0, count=SLICE):
+            columns = slice((i * SLICE + first) // PER_COLUMN, (i * SLICE + first + count) // PER_COLUMN)
+            nc.vector.tensor_copy(grouped[i][:, first : first + count, t], x_f32[:, t, :].indirect(offsets[:, columns]))
 
         def scalar_gather(i, t):
             nc.scalar.activation(
@@ -99,33 +122,40 @@ def tile_routed_moe_kernel(tc, xT, w_words, w_scales, gate, offs, out):
                 mybir.ActivationFunctionType.Copy,
             )
 
-        def quantize_and_multiply(i):
+        def quantize(i, first=0, count=SLICE):
             nc.vector.quantize_mx(
-                out=x_code[i][:].bitcast(FP8X4),
-                scales=x_scale[i][:],
-                in_=grouped[i][:].rearrange("p j t -> p (j t)"),
+                out=x_code[i][:, first : first + count].bitcast(FP8X4),
+                scales=x_scale[i][:, first : first + count],
+                in_=grouped[i][:, first : first + count, :].rearrange("p j t -> p (j t)"),
             )
+
+        def multiply(e, h):
+            i = e * C // SLICE
+            in_slice = e * C - i * SLICE
+            features = slice(h * P, (h + 1) * P)
+            nc.tensor.matmul_mx(
+                out=bank_of[e, h],
+                lhsT=w_code[:, e, features].bitcast(FP8X4),
+                lhsT_scale=w_scale[:, e, features],
+                rhs=x_code[i][:, in_slice : in_slice + C].bitcast(FP8X4),
+                rhs_scale=x_scale[i][:, in_slice : in_slice + C],
+                start=True,
+                stop=True,
+            )
+
+        def quantize_and_multiply(i):
+            quantize(i)
             for h in range(FEATURE_BLOCKS):
                 for e in range(i * SLICE // C, (i + 1) * SLICE // C):
-                    features = slice(h * P, (h + 1) * P)
-                    in_slice = e * C - i * SLICE
-                    nc.tensor.matmul_mx(
-                        out=sums[i][h][:, in_slice : in_slice + C],
-                        lhsT=w_code[:, e, features].bitcast(FP8X4),
-                        lhsT_scale=w_scale[:, e, features],
-                        rhs=x_code[i][:, in_slice : in_slice + C].bitcast(FP8X4),
-                        rhs_scale=x_scale[i][:, in_slice : in_slice + C],
-                        start=True,
-                        stop=True,
-                    )
+                    multiply(e, h)
 
         def copy_sums(i, h):
-            nc.scalar.copy(sums_sb[i, h][:], sums[i][h][:])
+            nc.scalar.copy(sums_sb[i, h], sums[i, h][:])
 
         def scatter(i, h):
             nc.vector.tensor_tensor(
                 windows[h][:].indirect(offsets[:, list_columns(i)]),
-                sums_sb[i, h][:],
+                sums_sb[i, h],
                 gate_of_slice[i, h],
                 mybir.AluOpType.mult,
             )
@@ -143,20 +173,30 @@ def tile_routed_moe_kernel(tc, xT, w_words, w_scales, gate, offs, out):
             grouped[i] = held.tile([P, SLICE, PACK], BF16, name="grouped%d" % i, align_bytes=MX_ALIGN)
         x_code[0] = held.tile([P, SLICE], U32, name="x_code0", align_bytes=MX_ALIGN)
         first_sums = [held.tile([P, C], F32, name="first_sums%d" % e, tag="slot_f%d" % e, align_bytes=MX_ALIGN) for e in range(2)]
-        sums_sb[0, 1] = held.tile([P, SLICE], F32, name="sums_sb0_1")
-        sums_sb[1, 0] = held.tile([P, SLICE], F32, name="sums_sb1_0", tag="slot_1", align_bytes=MX_ALIGN)
-        sums_sb[1, 1] = held.tile([P, SLICE], F32, name="sums_sb1_1")
-        for i in (2, 3):
-            for h in range(FEATURE_BLOCKS):
-                sums_sb[i, h] = held.tile([P, SLICE], F32, name="sums_sb%d_%d" % (i, h))
+        sums_sb01 = held.tile([P, SLICE], F32, name="sums_sb01")
+        sums_sb10 = held.tile([P, SLICE], F32, name="sums_sb10", tag="slot_1", align_bytes=MX_ALIGN)
+        sums_sb11 = held.tile([P, SLICE], F32, name="sums_sb11")
+        sums_sb20 = held.tile([P, SLICE], F32, name="sums_sb20")
+        sums_sb21 = held.tile([P, SLICE], F32, name="sums_sb21")
+        sums_sb3 = held.tile([P, FEATURE_BLOCKS, SLICE], F32, name="sums_sb3")
+        sums_sb[0, 1], sums_sb[1, 0], sums_sb[1, 1] = sums_sb01[:], sums_sb10[:], sums_sb11[:]
+        sums_sb[2, 0], sums_sb[2, 1] = sums_sb20[:], sums_sb21[:]
+        for h in range(FEATURE_BLOCKS):
+            sums_sb[3, h] = sums_sb3[:, h, :]
 
-        for t in range(PACK):
+        for t in range(PACK - 1):
             vector_gather(0, t)
             scalar_gather(1, t)
             scalar_gather(2, t)
-        quantize_and_multiply(0)
         for e in range(2):
-            nc.vector.tensor_copy(first_sums[e][:], sums[0][0][:, e * C : (e + 1) * C])
+            vector_gather(0, PACK - 1, e * C, C)
+            quantize(0, e * C, C)
+            for h in range(FEATURE_BLOCKS):
+                multiply(e, h)
+        scalar_gather(1, PACK - 1)
+        scalar_gather(2, PACK - 1)
+        for e in range(2):
+            nc.vector.tensor_copy(first_sums[e][:], first_bank[e][:])
         copy_sums(0, 1)
         for e in range(2):
             first_scatter(e)
@@ -176,8 +216,7 @@ def tile_routed_moe_kernel(tc, xT, w_words, w_scales, gate, offs, out):
         scatter(1, 1)
         x_code[3] = held.tile([P, SLICE], U32, name="x_code3", tag="slot_1", align_bytes=MX_ALIGN)
         quantize_and_multiply(3)
-        copy_sums(3, 0)
-        copy_sums(3, 1)
+        nc.scalar.copy(sums_sb3[:].rearrange("p h j -> p (h j)"), last_bank[:].rearrange("p h j -> p (h j)"))
         for i in (2, 3):
             for h in range(FEATURE_BLOCKS):
                 scatter(i, h)

@@ -52,11 +52,14 @@ def tile_routed_moe_kernel(tc, xT, w_words, w_scales, gate, offs, out):
         w_words_by_partition = w_words.rearrange("e a p n r -> p (e a) (n r)").bitcast(I32)
         gate_by_partition = gate.rearrange("(h p) j -> p h j", p=P)
         gate_of_slice = {}
-        for quadrant in range(P // QUADRANT):
-            nc.sync.dma_start(
-                w_scale[QUADRANT * quadrant : QUADRANT * quadrant + SCALE_ROWS, :, :].bitcast(I32),
-                w_scales[:, 0, SCALE_ROWS * quadrant : SCALE_ROWS * (quadrant + 1), :].rearrange("e q n -> q e n").bitcast(I32),
-            )
+        def load_scales(first, count):
+            experts = slice(first * SLICE // C, (first + count) * SLICE // C)
+            for quadrant in range(P // QUADRANT):
+                nc.sync.dma_start(
+                    w_scale[QUADRANT * quadrant : QUADRANT * quadrant + SCALE_ROWS, experts, :].bitcast(I32),
+                    w_scales[experts, 0, SCALE_ROWS * quadrant : SCALE_ROWS * (quadrant + 1), :].rearrange("e q n -> q e n").bitcast(I32),
+                )
+
         def load_codes(first, count, features=slice(0, N)):
             experts = slice(first * SLICE // C, (first + count) * SLICE // C)
             nc.sync.dma_start(w_code[:, experts, features].bitcast(I32), w_words_by_partition[:, experts, features])
@@ -68,10 +71,12 @@ def tile_routed_moe_kernel(tc, xT, w_words, w_scales, gate, offs, out):
                 for k, h in enumerate(blocks):
                     gate_of_slice[first + place, h] = tile[:, k, place * SLICE : (place + 1) * SLICE]
 
+        load_scales(0, 1)
         load_codes(0, 1, slice(0, P))
         load_gate(0, 1, (0,))
         load_codes(0, 1, slice(P, N))
         load_gate(0, 1, (1,))
+        load_scales(1, 3)
         load_codes(1, 1)
         load_gate(1, 1, (0, 1))
         load_codes(2, 2)

@@ -19,12 +19,13 @@ QUADRANT = 32
 SCALE_ROWS = QUADRANT // 8
 MX_ALIGN = 64
 SLOTS = E * C
-FEATURE_BLOCKS = N // P
+BLOCKS = N // P
 PER_COLUMN = 16
 
-SLICE = 2 * C
+PAIR = 2
+SLICE = PAIR * C
 SLICES = SLOTS // SLICE
-LOAD_GROUPS = ((0,), (1,), (2, 3))
+LAST = SLICES - 1
 
 
 def tile_routed_moe_kernel(tc, xT, w_words, w_scales, gate, offs, out):
@@ -34,49 +35,58 @@ def tile_routed_moe_kernel(tc, xT, w_words, w_scales, gate, offs, out):
         held = ctx.enter_context(tc.tile_pool(name="held", bufs=1))
         psum = ctx.enter_context(tc.psum_pool(name="psum", bufs=1))
 
-        def list_columns(i):
-            per_slice = SLICE // PER_COLUMN
-            return slice(i * per_slice, (i + 1) * per_slice)
+        def list_columns(first_slot, count):
+            return slice(first_slot // PER_COLUMN, (first_slot + count) // PER_COLUMN)
+
+        def experts_of(i):
+            return range(i * PAIR, (i + 1) * PAIR)
+
+        def expert_run(first_slice, count):
+            return slice(first_slice * PAIR, (first_slice + count) * PAIR)
 
         offsets = lists.tile([P, SLOTS // PER_COLUMN], U16, name="offsets")
-        nc.sync.dma_start(offsets[:], offs)
-
         x_f32 = held.tile([P, PACK, T], F32, name="x_f32")
         x_planes = xT.rearrange("(p t) m -> p t m", t=PACK)
         for t in range(PACK):
             nc.sync.dma_start(x_f32[:, t, :], x_planes[:, t, :])
+            if t == 0:
+                nc.sync.dma_start(offsets[:], offs)
 
         w_code = held.tile([P, E, N], U32, name="w_code", align_bytes=MX_ALIGN)
         w_scale = held.tile([P, E, N], U8, name="w_scale", align_bytes=MX_ALIGN)
         nc.vector.memset(w_scale[:].rearrange("p e n -> p (e n)").bitcast(I32), 0)
         w_words_by_partition = w_words.rearrange("e a p n r -> p (e a) (n r)").bitcast(I32)
         gate_by_partition = gate.rearrange("(h p) j -> p h j", p=P)
-        gate_of_slice = {}
-        def load_scales(first, count):
-            experts = slice(first * SLICE // C, (first + count) * SLICE // C)
+        gate_sb = {}
+
+        def load_scales(first_slice, count):
+            experts = expert_run(first_slice, count)
             for quadrant in range(P // QUADRANT):
                 nc.sync.dma_start(
                     w_scale[QUADRANT * quadrant : QUADRANT * quadrant + SCALE_ROWS, experts, :].bitcast(I32),
                     w_scales[experts, 0, SCALE_ROWS * quadrant : SCALE_ROWS * (quadrant + 1), :].rearrange("e q n -> q e n").bitcast(I32),
                 )
 
-        def load_codes(first, count, features=slice(0, N)):
-            experts = slice(first * SLICE // C, (first + count) * SLICE // C)
+        def load_codes(first_slice, count, features=slice(0, N)):
+            experts = expert_run(first_slice, count)
             nc.sync.dma_start(w_code[:, experts, features].bitcast(I32), w_words_by_partition[:, experts, features])
 
-        def load_gate(first, count, blocks):
-            tile = held.tile([P, len(blocks), count * SLICE], F32, name="gate%d_%d" % (first, blocks[0]), tag="gate%d_%d" % (first, blocks[0]), align_bytes=MX_ALIGN)
-            nc.sync.dma_start(tile[:], gate_by_partition[:, blocks[0] : blocks[-1] + 1, first * SLICE : (first + count) * SLICE])
+        def load_gate(first_slice, count, blocks):
+            name = "gate%d_%d" % (first_slice, blocks[0])
+            loaded = held.tile([P, len(blocks), count * SLICE], F32, name=name, tag=name, align_bytes=MX_ALIGN)
+            nc.sync.dma_start(
+                loaded[:], gate_by_partition[:, blocks[0] : blocks[-1] + 1, first_slice * SLICE : (first_slice + count) * SLICE]
+            )
             for place in range(count):
                 for k, h in enumerate(blocks):
-                    gate_of_slice[first + place, h] = tile[:, k, place * SLICE : (place + 1) * SLICE]
+                    gate_sb[first_slice + place, h] = loaded[:, k, place * SLICE : (place + 1) * SLICE]
 
         load_scales(0, 1)
         load_codes(0, 1, slice(0, P))
         load_gate(0, 1, (0,))
         load_codes(0, 1, slice(P, N))
         load_gate(0, 1, (1,))
-        load_scales(1, 3)
+        load_scales(1, SLICES - 1)
         load_codes(1, 1)
         load_gate(1, 1, (0, 1))
         load_codes(2, 2)
@@ -92,38 +102,39 @@ def tile_routed_moe_kernel(tc, xT, w_words, w_scales, gate, offs, out):
             nc.gpsimd.tensor_copy(x_bf16[:, t, :], x_f32[:, t, :])
 
         grouped = {}
-        sums_sb = {}
         x_code = {}
         x_scale = [held.tile([P, SLICE], U8, name="x_scale%d" % i, align_bytes=MX_ALIGN) for i in range(SLICES)]
-        windows = [held.tile([P, T], F32, name="window%d" % h) for h in range(FEATURE_BLOCKS)]
+        windows = [held.tile([P, T], F32, name="window%d" % h) for h in range(BLOCKS)]
 
-        bank_of = {}
-        first_bank = [psum.tile([P, C], F32, name="first_bank%d" % e) for e in range(2)]
-        sums = {}
-        sums[0, 1] = psum.tile([P, SLICE], F32, name="sums0_1")
-        for i in (1, 2):
-            for h in range(FEATURE_BLOCKS):
-                sums[i, h] = psum.tile([P, SLICE], F32, name="sums%d_%d" % (i, h))
-        last_bank = psum.tile([P, FEATURE_BLOCKS, SLICE], F32, name="last_bank")
+        first_bank = [psum.tile([P, C], F32, name="first_bank%d" % e) for e in experts_of(0)]
+        bank = {}
+        bank[0, 1] = psum.tile([P, SLICE], F32, name="bank0_1")
+        for i in range(1, LAST):
+            for h in range(BLOCKS):
+                bank[i, h] = psum.tile([P, SLICE], F32, name="bank%d_%d" % (i, h))
+        last_bank = psum.tile([P, BLOCKS, SLICE], F32, name="last_bank")
+        sums_of = {}
         for e in range(E):
-            i = e * C // SLICE
-            in_slice = e * C - i * SLICE
-            for h in range(FEATURE_BLOCKS):
+            i = e // PAIR
+            in_slice = slice((e - i * PAIR) * C, (e - i * PAIR + 1) * C)
+            for h in range(BLOCKS):
                 if i == 0 and h == 0:
-                    bank_of[e, h] = first_bank[e][:]
-                elif i == SLICES - 1:
-                    bank_of[e, h] = last_bank[:, h, in_slice : in_slice + C]
+                    sums_of[e, h] = first_bank[e][:]
+                elif i == LAST:
+                    sums_of[e, h] = last_bank[:, h, in_slice]
                 else:
-                    bank_of[e, h] = sums[i, h][:, in_slice : in_slice + C]
+                    sums_of[e, h] = bank[i, h][:, in_slice]
 
         def vector_gather(i, t, first=0, count=SLICE):
-            columns = slice((i * SLICE + first) // PER_COLUMN, (i * SLICE + first + count) // PER_COLUMN)
-            nc.vector.tensor_copy(grouped[i][:, first : first + count, t], x_f32[:, t, :].indirect(offsets[:, columns]))
+            nc.vector.tensor_copy(
+                grouped[i][:, first : first + count, t],
+                x_f32[:, t, :].indirect(offsets[:, list_columns(i * SLICE + first, count)]),
+            )
 
         def scalar_gather(i, t):
             nc.scalar.activation(
                 grouped[i][:, :, t],
-                x_bf16[:, t, :].indirect(offsets[:, list_columns(i)]),
+                x_bf16[:, t, :].indirect(offsets[:, list_columns(i * SLICE, SLICE)]),
                 mybir.ActivationFunctionType.Copy,
             )
 
@@ -135,95 +146,85 @@ def tile_routed_moe_kernel(tc, xT, w_words, w_scales, gate, offs, out):
             )
 
         def multiply(e, h):
-            i = e * C // SLICE
-            in_slice = e * C - i * SLICE
+            i = e // PAIR
+            in_slice = slice((e - i * PAIR) * C, (e - i * PAIR + 1) * C)
             features = slice(h * P, (h + 1) * P)
             nc.tensor.matmul_mx(
-                out=bank_of[e, h],
+                out=sums_of[e, h],
                 lhsT=w_code[:, e, features].bitcast(FP8X4),
                 lhsT_scale=w_scale[:, e, features],
-                rhs=x_code[i][:, in_slice : in_slice + C].bitcast(FP8X4),
-                rhs_scale=x_scale[i][:, in_slice : in_slice + C],
+                rhs=x_code[i][:, in_slice].bitcast(FP8X4),
+                rhs_scale=x_scale[i][:, in_slice],
                 start=True,
                 stop=True,
             )
 
         def quantize_and_multiply(i):
             quantize(i)
-            for h in range(FEATURE_BLOCKS):
-                for e in range(i * SLICE // C, (i + 1) * SLICE // C):
+            for h in range(BLOCKS):
+                for e in experts_of(i):
                     multiply(e, h)
 
-        def copy_sums(i, h):
-            nc.scalar.copy(sums_sb[i, h], sums[i, h][:])
+        def copy_bank(i, h):
+            nc.scalar.copy(sums_sb[i, h], bank[i, h][:])
 
-        def scatter(i, h):
+        def scatter(h, first_slot, count, sums, gate_columns):
             nc.vector.tensor_tensor(
-                windows[h][:].indirect(offsets[:, list_columns(i)]),
-                sums_sb[i, h],
-                gate_of_slice[i, h],
-                mybir.AluOpType.mult,
+                windows[h][:].indirect(offsets[:, list_columns(first_slot, count)]), sums, gate_columns, mybir.AluOpType.mult
             )
 
-        def first_scatter(e):
-            per_expert = C // PER_COLUMN
-            nc.vector.tensor_tensor(
-                windows[0][:].indirect(offsets[:, e * per_expert : (e + 1) * per_expert]),
-                first_sums[e][:],
-                gate_of_slice[0, 0][:, e * C : (e + 1) * C],
-                mybir.AluOpType.mult,
-            )
+        def scatter_slice(i, h):
+            scatter(h, i * SLICE, SLICE, sums_sb[i, h], gate_sb[i, h])
 
-        for i in range(3):
+        for i in range(LAST):
             grouped[i] = held.tile([P, SLICE, PACK], BF16, name="grouped%d" % i, align_bytes=MX_ALIGN)
         x_code[0] = held.tile([P, SLICE], U32, name="x_code0", align_bytes=MX_ALIGN)
-        first_sums = [held.tile([P, C], F32, name="first_sums%d" % e, tag="slot_f%d" % e, align_bytes=MX_ALIGN) for e in range(2)]
-        sums_sb01 = held.tile([P, SLICE], F32, name="sums_sb01")
-        sums_sb10 = held.tile([P, SLICE], F32, name="sums_sb10", tag="slot_1", align_bytes=MX_ALIGN)
-        sums_sb11 = held.tile([P, SLICE], F32, name="sums_sb11")
-        sums_sb20 = held.tile([P, SLICE], F32, name="sums_sb20")
-        sums_sb21 = held.tile([P, SLICE], F32, name="sums_sb21")
-        sums_sb3 = held.tile([P, FEATURE_BLOCKS, SLICE], F32, name="sums_sb3")
-        sums_sb[0, 1], sums_sb[1, 0], sums_sb[1, 1] = sums_sb01[:], sums_sb10[:], sums_sb11[:]
-        sums_sb[2, 0], sums_sb[2, 1] = sums_sb20[:], sums_sb21[:]
-        for h in range(FEATURE_BLOCKS):
-            sums_sb[3, h] = sums_sb3[:, h, :]
+        first_sums = [held.tile([P, C], F32, name="first_sums%d" % e, tag="first_sums%d" % e, align_bytes=MX_ALIGN) for e in experts_of(0)]
+        sums_sb = {}
+        for i, h in sorted(bank):
+            name = "sums_sb%d_%d" % (i, h)
+            copied = held.tile([P, SLICE], F32, name=name, tag=name, align_bytes=MX_ALIGN)
+            sums_sb[i, h] = copied[:]
+        last_sums = held.tile([P, BLOCKS, SLICE], F32, name="last_sums")
+        for h in range(BLOCKS):
+            sums_sb[LAST, h] = last_sums[:, h, :]
 
         for t in range(PACK - 1):
             vector_gather(0, t)
             scalar_gather(1, t)
             scalar_gather(2, t)
-        for e in range(2):
+        for e in experts_of(0):
             vector_gather(0, PACK - 1, e * C, C)
             quantize(0, e * C, C)
-            for h in range(FEATURE_BLOCKS):
+            for h in range(BLOCKS):
                 multiply(e, h)
         scalar_gather(1, PACK - 1)
         scalar_gather(2, PACK - 1)
-        for e in range(2):
+
+        for e in experts_of(0):
             nc.vector.tensor_copy(first_sums[e][:], first_bank[e][:])
-        copy_sums(0, 1)
-        for e in range(2):
-            first_scatter(e)
-        x_code[1] = held.tile([P, SLICE], U32, name="x_code1", tag="slot_f0", align_bytes=MX_ALIGN)
+        copy_bank(0, 1)
+        for e in experts_of(0):
+            scatter(0, e * C, C, first_sums[e][:], gate_sb[0, 0][:, e * C : (e + 1) * C])
+        x_code[1] = held.tile([P, SLICE], U32, name="x_code1", tag="first_sums0", align_bytes=MX_ALIGN)
         quantize_and_multiply(1)
-        x_code[2] = held.tile([P, SLICE], U32, name="x_code2", tag="slot_f1", align_bytes=MX_ALIGN)
+        x_code[2] = held.tile([P, SLICE], U32, name="x_code2", tag="first_sums1", align_bytes=MX_ALIGN)
         quantize_and_multiply(2)
-        scatter(0, 1)
-        copy_sums(1, 0)
-        copy_sums(1, 1)
-        grouped[3] = held.tile([P, SLICE, PACK], BF16, name="grouped3", tag="slot_f0", align_bytes=MX_ALIGN)
+        scatter_slice(0, 1)
+        copy_bank(1, 0)
+        copy_bank(1, 1)
+        grouped[LAST] = held.tile([P, SLICE, PACK], BF16, name="grouped%d" % LAST, tag="first_sums0", align_bytes=MX_ALIGN)
         for t in range(PACK):
-            scalar_gather(3, t)
-        copy_sums(2, 0)
-        copy_sums(2, 1)
-        scatter(1, 0)
-        scatter(1, 1)
-        x_code[3] = held.tile([P, SLICE], U32, name="x_code3", tag="slot_1", align_bytes=MX_ALIGN)
-        quantize_and_multiply(3)
-        nc.scalar.copy(sums_sb3[:].rearrange("p h j -> p (h j)"), last_bank[:].rearrange("p h j -> p (h j)"))
-        for i in (2, 3):
-            for h in range(FEATURE_BLOCKS):
-                scatter(i, h)
-        for h in range(FEATURE_BLOCKS):
+            scalar_gather(LAST, t)
+        copy_bank(2, 0)
+        copy_bank(2, 1)
+        scatter_slice(1, 0)
+        scatter_slice(1, 1)
+        x_code[LAST] = held.tile([P, SLICE], U32, name="x_code%d" % LAST, tag="sums_sb1_0", align_bytes=MX_ALIGN)
+        quantize_and_multiply(LAST)
+        nc.scalar.copy(last_sums[:].rearrange("p h j -> p (h j)"), last_bank[:].rearrange("p h j -> p (h j)"))
+        for i in range(2, SLICES):
+            for h in range(BLOCKS):
+                scatter_slice(i, h)
+        for h in range(BLOCKS):
             nc.sync.dma_start(out[h * P : (h + 1) * P, :], windows[h][:])

@@ -83,9 +83,8 @@ def tile_routed_moe_kernel(tc, xT, w_words, w_scales, gate, offs, out):
 
         load_scales(0, 1)
         load_codes(0, 1, slice(0, P))
-        load_gate(0, 1, (0,))
         load_codes(0, 1, slice(P, N))
-        load_gate(0, 1, (1,))
+        load_gate(0, 1, (0, 1))
         load_scales(1, SLICES - 1)
         load_codes(1, 1)
         load_gate(1, 1, (0, 1))
@@ -106,9 +105,9 @@ def tile_routed_moe_kernel(tc, xT, w_words, w_scales, gate, offs, out):
         x_scale = [held.tile([P, SLICE], U8, name="x_scale%d" % i, align_bytes=MX_ALIGN) for i in range(SLICES)]
         windows = [held.tile([P, T], F32, name="window%d" % h) for h in range(BLOCKS)]
 
-        first_bank = [psum.tile([P, C], F32, name="first_bank%d" % e) for e in experts_of(0)]
+        first_bank = [psum.tile([P, C], F32, name="first_bank%d" % h) for h in range(BLOCKS)]
+        second_bank = psum.tile([P, BLOCKS, C], F32, name="second_bank")
         bank = {}
-        bank[0, 1] = psum.tile([P, SLICE], F32, name="bank0_1")
         for i in range(1, LAST):
             for h in range(BLOCKS):
                 bank[i, h] = psum.tile([P, SLICE], F32, name="bank%d_%d" % (i, h))
@@ -118,8 +117,10 @@ def tile_routed_moe_kernel(tc, xT, w_words, w_scales, gate, offs, out):
             i = e // PAIR
             in_slice = slice((e - i * PAIR) * C, (e - i * PAIR + 1) * C)
             for h in range(BLOCKS):
-                if i == 0 and h == 0:
-                    sums_of[e, h] = first_bank[e][:]
+                if e == 0:
+                    sums_of[e, h] = first_bank[h][:]
+                elif e == 1:
+                    sums_of[e, h] = second_bank[:, h, :]
                 elif i == LAST:
                     sums_of[e, h] = last_bank[:, h, in_slice]
                 else:
@@ -179,7 +180,8 @@ def tile_routed_moe_kernel(tc, xT, w_words, w_scales, gate, offs, out):
         for i in range(LAST):
             grouped[i] = held.tile([P, SLICE, PACK], BF16, name="grouped%d" % i, align_bytes=MX_ALIGN)
         x_code[0] = held.tile([P, SLICE], U32, name="x_code0", align_bytes=MX_ALIGN)
-        first_sums = [held.tile([P, C], F32, name="first_sums%d" % e, tag="first_sums%d" % e, align_bytes=MX_ALIGN) for e in experts_of(0)]
+        first_sums = [held.tile([P, C], F32, name="first_sums%d" % h, tag="first_sums%d" % h, align_bytes=MX_ALIGN) for h in range(BLOCKS)]
+        second_sums = held.tile([P, BLOCKS, C], F32, name="second_sums", align_bytes=MX_ALIGN)
         sums_sb = {}
         for i, h in sorted(bank):
             name = "sums_sb%d_%d" % (i, h)
@@ -201,16 +203,17 @@ def tile_routed_moe_kernel(tc, xT, w_words, w_scales, gate, offs, out):
         scalar_gather(1, PACK - 1)
         scalar_gather(2, PACK - 1)
 
-        for e in experts_of(0):
-            nc.vector.tensor_copy(first_sums[e][:], first_bank[e][:])
-        copy_bank(0, 1)
-        for e in experts_of(0):
-            scatter(0, e * C, C, first_sums[e][:], gate_sb[0, 0][:, e * C : (e + 1) * C])
+        for h in range(BLOCKS):
+            nc.vector.tensor_copy(first_sums[h][:], first_bank[h][:])
+        nc.scalar.copy(second_sums[:].rearrange("p h j -> p (h j)"), second_bank[:].rearrange("p h j -> p (h j)"))
+        for h in range(BLOCKS):
+            scatter(h, 0, C, first_sums[h][:], gate_sb[0, h][:, 0:C])
         x_code[1] = held.tile([P, SLICE], U32, name="x_code1", tag="first_sums0", align_bytes=MX_ALIGN)
         quantize_and_multiply(1)
         x_code[2] = held.tile([P, SLICE], U32, name="x_code2", tag="first_sums1", align_bytes=MX_ALIGN)
         quantize_and_multiply(2)
-        scatter_slice(0, 1)
+        for h in range(BLOCKS):
+            scatter(h, C, C, second_sums[:, h, :], gate_sb[0, h][:, C : 2 * C])
         copy_bank(1, 0)
         copy_bank(1, 1)
         grouped[LAST] = held.tile([P, SLICE, PACK], BF16, name="grouped%d" % LAST, tag="first_sums0", align_bytes=MX_ALIGN)

@@ -48,7 +48,12 @@ def tile_routed_moe_kernel(tc, xT, w_words, w_scales, gate, offs, out):
         x_f32 = held.tile([P, PACK, T], F32, name="x_f32")
         x_planes = xT.rearrange("(p t) m -> p t m", t=PACK)
         for t in range(PACK):
-            nc.sync.dma_start(x_f32[:, t, :], x_planes[:, t, :])
+            if t == 1:
+                for half in range(2):
+                    columns = slice(half * (T // 2), (half + 1) * (T // 2))
+                    nc.sync.dma_start(x_f32[:, t, columns], x_planes[:, t, columns])
+            else:
+                nc.sync.dma_start(x_f32[:, t, :], x_planes[:, t, :])
             if t == 0:
                 nc.sync.dma_start(offsets[:], offs)
 
@@ -98,7 +103,12 @@ def tile_routed_moe_kernel(tc, xT, w_words, w_scales, gate, offs, out):
         x_bf16 = held.tile([P, PACK, T], BF16, name="x_bf16")
         nc.vector.tensor_copy(x_bf16[:, 0, :], x_f32[:, 0, :])
         for t in range(1, PACK):
-            nc.gpsimd.tensor_copy(x_bf16[:, t, :], x_f32[:, t, :])
+            if t == 1:
+                for half in range(2):
+                    columns = slice(half * (T // 2), (half + 1) * (T // 2))
+                    nc.gpsimd.tensor_copy(x_bf16[:, t, columns], x_f32[:, t, columns])
+            else:
+                nc.gpsimd.tensor_copy(x_bf16[:, t, :], x_f32[:, t, :])
 
         grouped = {}
         x_code = {}

@@ -48,7 +48,7 @@ def tile_routed_moe_kernel(tc, xT, w_words, w_scales, gate, offs, out):
         x_f32 = held.tile([P, PACK, T], F32, name="x_f32")
         x_planes = xT.rearrange("(p t) m -> p t m", t=PACK)
         for t in range(PACK):
-            if t == 1:
+            if t >= 1:
                 for half in range(2):
                     columns = slice(half * (T // 2), (half + 1) * (T // 2))
                     nc.sync.dma_start(x_f32[:, t, columns], x_planes[:, t, columns])
@@ -103,7 +103,7 @@ def tile_routed_moe_kernel(tc, xT, w_words, w_scales, gate, offs, out):
         x_bf16 = held.tile([P, PACK, T], BF16, name="x_bf16")
         nc.vector.tensor_copy(x_bf16[:, 0, :], x_f32[:, 0, :])
         for t in range(1, PACK):
-            if t == 1:
+            if t >= 1:
                 for half in range(2):
                     columns = slice(half * (T // 2), (half + 1) * (T // 2))
                     nc.gpsimd.tensor_copy(x_bf16[:, t, columns], x_f32[:, t, columns])

@@ -48,7 +48,7 @@ def tile_routed_moe_kernel(tc, xT, w_words, w_scales, gate, offs, out):
         x_f32 = held.tile([P, PACK, T], F32, name="x_f32")
         x_planes = xT.rearrange("(p t) m -> p t m", t=PACK)
         for t in range(PACK):
-            if t >= 1:
+            if t in (1, 2):
                 for half in range(2):
                     columns = slice(half * (T // 2), (half + 1) * (T // 2))
                     nc.sync.dma_start(x_f32[:, t, columns], x_planes[:, t, columns])
@@ -103,7 +103,7 @@ def tile_routed_moe_kernel(tc, xT, w_words, w_scales, gate, offs, out):
         x_bf16 = held.tile([P, PACK, T], BF16, name="x_bf16")
         nc.vector.tensor_copy(x_bf16[:, 0, :], x_f32[:, 0, :])
         for t in range(1, PACK):
-            if t >= 1:
+            if t in (1, 2):
                 for half in range(2):
                     columns = slice(half * (T // 2), (half + 1) * (T // 2))
                     nc.gpsimd.tensor_copy(x_bf16[:, t, columns], x_f32[:, t, columns])

from contextlib import ExitStack

import concourse.mybir as mybir

K, T, E, C, N = 512, 1024, 8, 128, 256
FLOPS = 2 * K * N * E * C

F32 = mybir.dt.float32
BF16 = mybir.dt.bfloat16
U32 = mybir.dt.uint32
I32 = mybir.dt.int32
U16 = mybir.dt.uint16
U8 = mybir.dt.uint8
FP8X4 = mybir.dt.float8_e4m3fn_x4

P = 128
PACK = 4
QUADRANT = 32
SCALE_ROWS = QUADRANT // 8
MX_ALIGN = 64
SLOTS = E * C
BLOCKS = N // P
PER_COLUMN = 16

PAIR = 2
SLICE = PAIR * C
SLICES = SLOTS // SLICE
LAST = SLICES - 1


def tile_routed_moe_kernel(tc, xT, w_words, w_scales, gate, offs, out):
    nc = tc.nc
    with ExitStack() as ctx:
        lists = ctx.enter_context(tc.tile_pool(name="lists", bufs=1))
        held = ctx.enter_context(tc.tile_pool(name="held", bufs=1))
        psum = ctx.enter_context(tc.psum_pool(name="psum", bufs=1))

        def list_columns(first_slot, count):
            return slice(first_slot // PER_COLUMN, (first_slot + count) // PER_COLUMN)

        def experts_of(i):
            return range(i * PAIR, (i + 1) * PAIR)

        def expert_run(first_slice, count):
            return slice(first_slice * PAIR, (first_slice + count) * PAIR)

        offsets = lists.tile([P, SLOTS // PER_COLUMN], U16, name="offsets")
        x_f32 = held.tile([P, PACK, T], F32, name="x_f32")
        x_planes = xT.rearrange("(p t) m -> p t m", t=PACK)
        for t in range(PACK):
            if t in (1, 2):
                for half in range(2):
                    columns = slice(half * (T // 2), (half + 1) * (T // 2))
                    nc.sync.dma_start(x_f32[:, t, columns], x_planes[:, t, columns])
            else:
                nc.sync.dma_start(x_f32[:, t, :], x_planes[:, t, :])
            if t == 0:
                nc.sync.dma_start(offsets[:], offs)

        w_code = held.tile([P, E, N], U32, name="w_code", align_bytes=MX_ALIGN)
        w_scale = held.tile([P, E, N], U8, name="w_scale", align_bytes=MX_ALIGN)
        nc.vector.memset(w_scale[:].rearrange("p e n -> p (e n)").bitcast(I32), 0)
        w_words_by_partition = w_words.rearrange("e a p n r -> p (e a) (n r)").bitcast(I32)
        gate_by_partition = gate.rearrange("(h p) j -> p h j", p=P)
        gate_sb = {}

        def load_scales(first_slice, count):
            experts = expert_run(first_slice, count)
            for quadrant in range(P // QUADRANT):
                nc.sync.dma_start(
                    w_scale[QUADRANT * quadrant : QUADRANT * quadrant + SCALE_ROWS, experts, :].bitcast(I32),
                    w_scales[experts, 0, SCALE_ROWS * quadrant : SCALE_ROWS * (quadrant + 1), :].rearrange("e q n -> q e n").bitcast(I32),
                )

        def load_codes(first_slice, count, features=slice(0, N)):
            experts = expert_run(first_slice, count)
            nc.sync.dma_start(w_code[:, experts, features].bitcast(I32), w_words_by_partition[:, experts, features])

        def load_gate(first_slice, count, blocks):
            name = "gate%d_%d" % (first_slice, blocks[0])
            loaded = held.tile([P, len(blocks), count * SLICE], F32, name=name, tag=name, align_bytes=MX_ALIGN)
            nc.sync.dma_start(
                loaded[:], gate_by_partition[:, blocks[0] : blocks[-1] + 1, first_slice * SLICE : (first_slice + count) * SLICE]
            )
            for place in range(count):
                for k, h in enumerate(blocks):
                    gate_sb[first_slice + place, h] = loaded[:, k, place * SLICE : (place + 1) * SLICE]

        load_scales(0, 1)
        load_codes(0, 1, slice(0, P))
        load_codes(0, 1, slice(P, N))
        load_gate(0, 1, (0, 1))
        load_scales(1, SLICES - 1)
        load_codes(1, 1)
        load_gate(1, 1, (0, 1))
        load_codes(2, 2)
        load_gate(2, 2, (0, 1))

        warm = held.tile([P, 2], F32, name="warm")
        nc.gpsimd.memset(warm[:, 0:1], 0.0)
        nc.scalar.activation(warm[:, 1:2], warm[:, 0:1], mybir.ActivationFunctionType.Copy)

        x_bf16 = held.tile([P, PACK, T], BF16, name="x_bf16")
        nc.vector.tensor_copy(x_bf16[:, 0, :], x_f32[:, 0, :])
        for t in range(1, PACK):
            if t in (1, 2):
                for half in range(2):
                    columns = slice(half * (T // 2), (half + 1) * (T // 2))
                    nc.gpsimd.tensor_copy(x_bf16[:, t, columns], x_f32[:, t, columns])
            else:
                nc.gpsimd.tensor_copy(x_bf16[:, t, :], x_f32[:, t, :])

        grouped = {}
        x_code = {}
        x_scale = [held.tile([P, SLICE], U8, name="x_scale%d" % i, align_bytes=MX_ALIGN) for i in range(SLICES)]
        windows = [held.tile([P, T], F32, name="window%d" % h) for h in range(BLOCKS)]

        first_bank = [psum.tile([P, C], F32, name="first_bank%d" % h) for h in range(BLOCKS)]
        second_bank = psum.tile([P, BLOCKS, C], F32, name="second_bank")
        bank = {}
        for i in range(1, LAST):
            for h in range(BLOCKS):
                bank[i, h] = psum.tile([P, SLICE], F32, name="bank%d_%d" % (i, h))
        last_bank = psum.tile([P, BLOCKS, SLICE], F32, name="last_bank")
        sums_of = {}
        for e in range(E):
            i = e // PAIR
            in_slice = slice((e - i * PAIR) * C, (e - i * PAIR + 1) * C)
            for h in range(BLOCKS):
                if e == 0:
                    sums_of[e, h] = first_bank[h][:]
                elif e == 1:
                    sums_of[e, h] = second_bank[:, h, :]
                elif i == LAST:
                    sums_of[e, h] = last_bank[:, h, in_slice]
                else:
                    sums_of[e, h] = bank[i, h][:, in_slice]

        def vector_gather(i, t, first=0, count=SLICE):
            nc.vector.tensor_copy(
                grouped[i][:, first : first + count, t],
                x_f32[:, t, :].indirect(offsets[:, list_columns(i * SLICE + first, count)]),
            )

        def scalar_gather(i, t):
            nc.scalar.activation(
                grouped[i][:, :, t],
                x_bf16[:, t, :].indirect(offsets[:, list_columns(i * SLICE, SLICE)]),
                mybir.ActivationFunctionType.Copy,
            )

        def quantize(i, first=0, count=SLICE):
            nc.vector.quantize_mx(
                out=x_code[i][:, first : first + count].bitcast(FP8X4),
                scales=x_scale[i][:, first : first + count],
                in_=grouped[i][:, first : first + count, :].rearrange("p j t -> p (j t)"),
            )

        def multiply(e, h):
            i = e // PAIR
            in_slice = slice((e - i * PAIR) * C, (e - i * PAIR + 1) * C)
            features = slice(h * P, (h + 1) * P)
            nc.tensor.matmul_mx(
                out=sums_of[e, h],
                lhsT=w_code[:, e, features].bitcast(FP8X4),
                lhsT_scale=w_scale[:, e, features],
                rhs=x_code[i][:, in_slice].bitcast(FP8X4),
                rhs_scale=x_scale[i][:, in_slice],
                start=True,
                stop=True,
            )

        def quantize_and_multiply(i):
            quantize(i)
            for h in range(BLOCKS):
                for e in experts_of(i):
                    multiply(e, h)

        def copy_bank(i, h):
            nc.scalar.copy(sums_sb[i, h], bank[i, h][:])

        def scatter(h, first_slot, count, sums, gate_columns):
            nc.vector.tensor_tensor(
                windows[h][:].indirect(offsets[:, list_columns(first_slot, count)]), sums, gate_columns, mybir.AluOpType.mult
            )

        def scatter_slice(i, h):
            scatter(h, i * SLICE, SLICE, sums_sb[i, h], gate_sb[i, h])

        for i in range(LAST):
            grouped[i] = held.tile([P, SLICE, PACK], BF16, name="grouped%d" % i, align_bytes=MX_ALIGN)
        x_code[0] = held.tile([P, SLICE], U32, name="x_code0", align_bytes=MX_ALIGN)
        first_sums = [held.tile([P, C], F32, name="first_sums%d" % h, tag="first_sums%d" % h, align_bytes=MX_ALIGN) for h in range(BLOCKS)]
        second_sums = held.tile([P, BLOCKS, C], F32, name="second_sums", align_bytes=MX_ALIGN)
        sums_sb = {}
        for i, h in sorted(bank):
            name = "sums_sb%d_%d" % (i, h)
            copied = held.tile([P, SLICE], F32, name=name, tag=name, align_bytes=MX_ALIGN)
            sums_sb[i, h] = copied[:]
        last_sums = held.tile([P, BLOCKS, SLICE], F32, name="last_sums")
        for h in range(BLOCKS):
            sums_sb[LAST, h] = last_sums[:, h, :]

        for t in range(PACK - 1):
            vector_gather(0, t)
            scalar_gather(1, t)
            scalar_gather(2, t)
        for e in experts_of(0):
            vector_gather(0, PACK - 1, e * C, C)
            quantize(0, e * C, C)
            for h in range(BLOCKS):
                multiply(e, h)
        scalar_gather(1, PACK - 1)
        scalar_gather(2, PACK - 1)

        for h in range(BLOCKS):
            nc.vector.tensor_copy(first_sums[h][:], first_bank[h][:])
        nc.scalar.copy(second_sums[:].rearrange("p h j -> p (h j)"), second_bank[:].rearrange("p h j -> p (h j)"))
        for h in range(BLOCKS):
            scatter(h, 0, C, first_sums[h][:], gate_sb[0, h][:, 0:C])
        x_code[1] = held.tile([P, SLICE], U32, name="x_code1", tag="first_sums0", align_bytes=MX_ALIGN)
        quantize_and_multiply(1)
        x_code[2] = held.tile([P, SLICE], U32, name="x_code2", tag="first_sums1", align_bytes=MX_ALIGN)
        quantize_and_multiply(2)
        for h in range(BLOCKS):
            scatter(h, C, C, second_sums[:, h, :], gate_sb[0, h][:, C : 2 * C])
        copy_bank(1, 0)
        copy_bank(1, 1)
        grouped[LAST] = held.tile([P, SLICE, PACK], BF16, name="grouped%d" % LAST, tag="first_sums0", align_bytes=MX_ALIGN)
        for t in range(PACK):
            scalar_gather(LAST, t)
        copy_bank(2, 0)
        copy_bank(2, 1)
        scatter_slice(1, 0)
        scatter_slice(1, 1)
        x_code[LAST] = held.tile([P, SLICE], U32, name="x_code%d" % LAST, tag="sums_sb1_0", align_bytes=MX_ALIGN)
        quantize_and_multiply(LAST)
        nc.scalar.copy(last_sums[:].rearrange("p h j -> p (h j)"), last_bank[:].rearrange("p h j -> p (h j)"))
        for i in range(2, SLICES):
            for h in range(BLOCKS):
                scatter_slice(i, h)
        for h in range(BLOCKS):
            nc.sync.dma_start(out[h * P : (h + 1) * P, :], windows[h][:])
